import numpy as np
import ml_dtypes


def mxq(x, axis, fmt="e4m3"):
    dtype, down = {"e4m3": (ml_dtypes.float8_e4m3fn, 7), "e5m2": (ml_dtypes.float8_e5m2, 14)}[fmt]
    v = np.moveaxis(np.asarray(x, np.float32).astype(ml_dtypes.bfloat16).astype(np.float64), axis, -1)
    blocks = v.reshape(v.shape[:-1] + (-1, 32))
    amax = np.abs(blocks).max(-1, keepdims=True)
    byte = np.maximum(np.where(amax > 0, np.frexp(amax)[1] - 1 + 127, 0) - down, 1)
    scale = np.exp2(byte - 127.0)
    codes = (blocks / scale).astype(np.float32).astype(dtype).astype(np.float64)
    return np.moveaxis((codes * scale).reshape(v.shape), -1, axis)


WIDE = False


def mx_kscale(k):
    if not WIDE:
        return np.ones(k)
    levels = np.array([10, -10, 5, -5, 0])
    if k % 512:
        return np.exp2(np.random.permutation(np.resize(levels, k // 32))).repeat(32)
    a = np.empty((k // 512, 16))
    for p in range(k // 512):
        a[p, :8] = np.random.permutation(np.resize(levels, 8))
        for g in range(8):
            far = levels[np.abs(levels - a[p, g]) >= 10]
            a[p, g + 8] = far[np.random.randint(len(far))]
    return np.exp2(a.ravel()).repeat(32)


def f64(x):
    return np.asarray(x).astype(np.float64)


def striped(idx):
    return np.tile(idx.reshape(-1, 16).T, (8, 1)).astype(np.uint16)


def unstriped(offs):
    return offs[:16].T.reshape(-1).astype(np.int64)


E2M1 = np.array([0.0, 0.5, 1.0, 1.5, 2.0, 3.0, 4.0, 6.0, -0.0, -0.5, -1.0, -1.5, -2.0, -3.0, -4.0, -6.0])


def pack_weight(w, fmt):
    k, n = w.shape
    w = f64(np.asarray(w, np.float32).astype(ml_dtypes.bfloat16)).reshape(k // 32, 32, n)
    amax = np.abs(w).max(1)
    if fmt == "e4m3":
        byte = np.frexp(amax)[1] - 1 + 127 - 7
    else:
        mant, ex = np.frexp(amax / 6.0)
        byte = np.where(mant > 0.5, ex, ex - 1) + 127
    byte = np.clip(np.where(amax > 0, byte, 1), 1, 254)
    scaled = (w * np.exp2(127.0 - byte)[:, None, :]).reshape(k, n).astype(np.float32)
    by_word = np.ascontiguousarray(scaled.reshape(k // 512, 128, 4, n).transpose(0, 1, 3, 2))
    if fmt == "e4m3":
        words = by_word.astype(ml_dtypes.float8_e4m3fn).view(np.uint8)
    else:
        c = by_word.astype(ml_dtypes.float4_e2m1fn).view(np.uint8) & 0xF
        words = (c[..., 0::2] | (c[..., 1::2] << 4)).reshape(k // 512, 128, 2 * n)
    return np.ascontiguousarray(words), np.ascontiguousarray(byte.astype(np.uint8).reshape(k // 512, 16, n))


def unpack_weight(words, scales, fmt):
    g, _, n = scales.shape
    words = np.ascontiguousarray(words).reshape(g, 128, n, -1)
    if fmt == "e4m3":
        vals = words.view(ml_dtypes.float8_e4m3fn).astype(np.float64)
    else:
        nib = np.empty((g, 128, n, 4), np.uint8)
        nib[..., 0::2] = words & 0xF
        nib[..., 1::2] = words >> 4
        vals = E2M1[nib]
    vals = vals * np.repeat(np.exp2(scales.astype(np.float64) - 127.0), 8, axis=1)[..., None]
    return vals.transpose(0, 1, 3, 2).reshape(g * 512, n)


def gelu(v):
    return 0.5 * v * (1.0 + np.tanh(np.sqrt(2.0 / np.pi) * (v + 0.044715 * v**3)))


K, H, T, S, P = 1024, 1024, 4096, 1024, 512

def setup_inputs():
    n = np.random.standard_normal
    s = mx_kscale(K)[:, None]
    u = mx_kscale(H)[:, None]
    d = {}
    d["tab_words"], d["tab_scales"] = pack_weight(n((K, T)) * s, "e2m1")
    d["offs"] = striped(np.random.permutation(T)[:S])
    d["pos1"] = striped(np.random.permutation(S)[:P])
    d["pos2"] = striped(np.random.permutation(S)[:P])
    d["w1"] = (1.5 * n((K, H)) / K ** 0.5 / s).astype(np.float32)
    d["w2_words"], d["w2_scales"] = pack_weight(1.5 * n((H, H)) / H ** 0.5 / u, "e2m1")
    d["w3"] = (0.7 * n((H, H)) / H ** 0.5 / u).astype(np.float32)
    d["gx"] = (np.exp(0.3 * n(H)) * u[:, 0]).astype(np.float32)
    d["gz"] = (np.exp(0.3 * n(H)) * u[:, 0]).astype(np.float32)
    return d

def reference(tab_words, tab_scales, offs, pos1, pos2, w1, w2_words, w2_scales, w3, gx, gz):
    v = unpack_weight(tab_words, tab_scales, "e2m1")[:, unstriped(offs)]
    w2 = unpack_weight(w2_words, w2_scales, "e2m1")
    h = mxq(f64(w1), 0, "e4m3").T @ v
    left = h[:, unstriped(pos1)]
    right = h[:, unstriped(pos2)]
    act = 0.5 * left * (1.0 + np.tanh(0.7978845608028654 * (left + 0.044715 * left * left * left)))
    x = mxq(act * f64(gx)[:, None], 0, "e4m3")
    apart = np.sqrt(1.0 + np.square(left - right))
    z = mxq(apart * f64(gz)[:, None], 0, "e4m3")
    y = w2.T @ x + mxq(f64(w3), 0, "e4m3").T @ z
    return left + y

@@ -1,0 +1,269 @@
+from contextlib import ExitStack
+
+import concourse.mybir as mybir
+
+K, H, T, S, M = 1024, 1024, 4096, 1024, 512
+FLOPS = 2 * K * H * S + 2 * 2 * H * H * M
+
+F32 = mybir.dt.float32
+BF16 = mybir.dt.bfloat16
+I32 = mybir.dt.int32
+U32 = mybir.dt.uint32
+U16 = mybir.dt.uint16
+U8 = mybir.dt.uint8
+FP8X4 = mybir.dt.float8_e4m3fn_x4
+FP4X4 = mybir.dt.float4_e2m1fn_x4
+ACT = mybir.ActivationFunctionType
+ALU = mybir.AluOpType
+
+P = 128
+PACK = 4
+PASS = P * PACK
+BANK = 512
+
+
+def tile_list_binaural_fitting_gains_kernel(
+    tc, tab_words, tab_scales, offs, pos1, pos2, w1, w2_words, w2_scales, w3, gx, gz, out
+):
+    nc = tc.nc
+    with ExitStack() as ctx:
+        keep = ctx.enter_context(tc.tile_pool(name="keep", bufs=1))
+        raw = ctx.enter_context(tc.tile_pool(name="raw", bufs=5))
+        rounded = ctx.enter_context(tc.tile_pool(name="rounded", bufs=5))
+        psum = ctx.enter_context(tc.psum_pool(name="psum", bufs=8))
+
+        def held(name, shape, dtype):
+            return keep.tile(shape, dtype, name=name, align_bytes=64)
+
+        offs_sb = keep.tile([P, S // 16], U16, name="offs_sb")
+        pos1_sb = keep.tile([P, M // 16], U16, name="pos1_sb")
+        pos2_sb = keep.tile([P, M // 16], U16, name="pos2_sb")
+        tab_w = [held("tab_w%d" % a, [P, T], U16) for a in range(2)]
+        tab_s = held("tab_s", [P, T], U8)
+        v_w = [held("v_w%d" % a, [P, S], U16) for a in range(2)]
+        v_s = [held("v_s%d" % a, [P, S], U8) for a in range(2)]
+        w2_raw = held("w2_raw", [P, 2 * H], U16)
+        w2_w = held("w2_w", [P, 2 * H], U16)
+        w2_sraw = held("w2_sraw", [P, H], U8)
+        w2_s = [held("w2_s%d" % a, [P, H], U8) for a in range(2)]
+        gx_sb = held("gx_sb", [P, 2, PACK], F32)
+        gz_sb = held("gz_sb", [P, 2, PACK], F32)
+        warm = held("warm", [P, 1], F32)
+
+        def load_scale_rows(queue, tile, scales, row0):
+            for q in range(4):
+                queue.dma_start(
+                    out=tile[32 * q + row0 : 32 * q + row0 + 8, :].bitcast(I32),
+                    in_=scales[:, 4 * q : 4 * q + 4, :].bitcast(I32),
+                )
+
+        def load_weight(w, name, a, b):
+            t = raw.tile([P, PACK, PASS], F32, name="raw")
+            nc.sync.dma_start(
+                out=t[:],
+                in_=w[PASS * a : PASS * (a + 1), PASS * b : PASS * (b + 1)].rearrange("(p j) c -> p j c", j=PACK),
+            )
+            return t
+
+        def round_weight(engine, src):
+            dst = rounded.tile([P, PACK * PASS], BF16, name="rounded", align_bytes=64)
+            o = dst[:].rearrange("p (t m j) -> p m j t", t=PACK, j=PACK)
+            i = src[:].rearrange("p j (m t) -> p m j t", t=PACK)
+            if engine == "scalar":
+                nc.scalar.copy(out=o, in_=i)
+            else:
+                nc.vector.tensor_copy(out=o, in_=i)
+            return dst
+
+        def quantize(name, src):
+            codes = held(name + "_c", [P, PASS], U32)
+            scales = held(name + "_s", [P, PASS], U8)
+            nc.vector.quantize_mx(out=codes[:].bitcast(FP8X4), scales=scales[:], in_=src[:])
+            return codes, scales
+
+        for q in range(4):
+            nc.vector.memset(tab_s[32 * q : 32 * q + 24, :].bitcast(I32), 0)
+        nc.gpsimd.memset(warm[:], 0.0)
+        nc.scalar.activation(out=warm[:], in_=warm[:], func=ACT.Gelu_apprx_tanh)
+        for a in range(2):
+            nc.gpsimd.memset(v_s[a][96:P, :].bitcast(I32), 0)
+        nc.gpsimd.memset(w2_sraw[:].bitcast(I32), 0)
+        nc.gpsimd.memset(w2_s[1][96:P, :].bitcast(I32), 0)
+
+        w1_raw = {}
+        w3_raw = {}
+        nc.sync.dma_start(offs_sb[:], offs)
+        load_scale_rows(nc.sync, tab_s, tab_scales, 24)
+        nc.sync.dma_start(out=tab_w[0][:].bitcast(I32), in_=tab_words[0].bitcast(I32))
+        nc.sync.dma_start(
+            out=w2_raw[:].bitcast(I32).rearrange("p (a c) -> p a c", a=2),
+            in_=w2_words.bitcast(I32).rearrange("a p c -> p a c"),
+        )
+        w1_raw[0, 0] = load_weight(w1, "w1", 0, 0)
+        nc.sync.dma_start(out=tab_w[1][:].bitcast(I32), in_=tab_words[1].bitcast(I32))
+        halves = []
+        for u in range(2):
+            piece = held("w1_half%d" % u, [P, PACK, PASS // 2], F32)
+            nc.sync.dma_start(
+                out=piece[:],
+                in_=w1[PASS : 2 * PASS, 256 * u : 256 * (u + 1)].rearrange("(p j) c -> p j c", j=PACK),
+            )
+            halves.append(piece)
+        nc.sync.dma_start(pos1_sb[:], pos1)
+        nc.sync.dma_start(pos2_sb[:], pos2)
+        w1_raw[0, 1] = load_weight(w1, "w1", 0, 1)
+        w1_raw[1, 1] = load_weight(w1, "w1", 1, 1)
+        load_scale_rows(nc.sync, w2_sraw, w2_scales, 0)
+        nc.sync.dma_start(out=gx_sb[:], in_=gx.rearrange("(b p t) -> p b t", p=P, t=PACK))
+        nc.sync.dma_start(out=gz_sb[:], in_=gz.rearrange("(b p t) -> p b t", p=P, t=PACK))
+        for a in range(2):
+            for b in range(2):
+                w3_raw[a, b] = load_weight(w3, "w3", a, b)
+
+        picked_s = held("picked_s", [P, S], U8)
+        nc.vector.tensor_copy(picked_s[:], tab_s[:].indirect(offs_sb[:]))
+        for a in range(2):
+            row0 = 24 + 4 * a
+            nc.scalar.dma_start(out=v_s[a][0 : P - row0, :].bitcast(I32), in_=picked_s[row0:P, :].bitcast(I32))
+        w1_q = {}
+        nc.vector.tensor_copy(v_w[0][:], tab_w[0][:].indirect(offs_sb[:]))
+        w1_q[0, 0] = quantize("w1_00", round_weight("scalar", w1_raw[0, 0]))
+        nc.vector.tensor_copy(v_w[1][:], tab_w[1][:].indirect(offs_sb[:]))
+        nc.vector.tensor_copy(
+            w2_w[:].rearrange("p (g t q) -> p g q t", t=PACK, q=P),
+            w2_raw[:].rearrange("p (g q t) -> p g q t", t=PACK, q=P),
+        )
+        last = rounded.tile([P, PACK * PASS], BF16, name="rounded", align_bytes=64)
+        last_view = last[:].rearrange("p (t m j) -> p m j t", t=PACK, j=PACK)
+        nc.scalar.copy(out=last_view[:, 0:64], in_=halves[0][:].rearrange("p j (m t) -> p m j t", t=PACK))
+        nc.vector.tensor_copy(out=last_view[:, 64:128], in_=halves[1][:].rearrange("p j (m t) -> p m j t", t=PACK))
+        w1_q[1, 0] = quantize("w1_10", last)
+
+        h = [keep.tile([P, S], F32, name="h%d" % i, tag="h%d" % i) for i in range(8)]
+
+        def stage1(b):
+            banks = {}
+            for t in range(PACK):
+                for half in range(2):
+                    banks[t, half] = psum.tile([P, BANK], F32, name="bank")
+            for a in range(2):
+                codes, scales = w1_q[a, b]
+                for t in range(PACK):
+                    for half in range(2):
+                        cols = slice(BANK * half, BANK * (half + 1))
+                        nc.tensor.matmul_mx(
+                            out=banks[t, half][:],
+                            lhsT=codes[:, P * t : P * (t + 1)].bitcast(FP8X4),
+                            lhsT_scale=scales[:, P * t : P * (t + 1)],
+                            rhs=v_w[a][:, cols].bitcast(FP4X4),
+                            rhs_scale=v_s[a][:, cols],
+                            start=(a == 0),
+                            stop=(a == 1),
+                        )
+            for t in range(PACK):
+                for half in range(2):
+                    nc.scalar.copy(out=h[PACK * b + t][:, BANK * half : BANK * (half + 1)], in_=banks[t, half][:])
+
+        w1_q[0, 1] = quantize("w1_01", round_weight("vector", w1_raw[0, 1]))
+        stage1(0)
+        w1_q[1, 1] = quantize("w1_11", round_weight("scalar", w1_raw[1, 1]))
+        stage1(1)
+
+        left = [held("left%d" % b, [P, PACK, M], F32) for b in range(2)]
+        diff = [held("diff%d" % b, [P, PACK, M], F32) for b in range(2)]
+        woven = [held("woven%d" % b, [P, M * PACK], F32) for b in range(2)]
+
+        def gather_left(b):
+            for t in range(PACK):
+                nc.vector.tensor_copy(left[b][:, t, :], h[PACK * b + t][:].indirect(pos1_sb[:]))
+
+        def gather_diff(b):
+            ds = {}
+            home = "spare" if b == 0 else "h2"
+            for t in (3, 0, 1, 2):
+                ds[t] = keep.tile([P, M], F32, name="d%d%d" % (b, t), tag=home)
+                nc.vector.tensor_tensor(ds[t][:], h[PACK * b + t][:].indirect(pos2_sb[:]), left[b][:, t, :], ALU.subtract)
+                home = "h%d" % (PACK * b + t)
+            return ds
+
+        def square(b, ds):
+            for t in (3, 0, 1, 2):
+                nc.scalar.activation(out=diff[b][:, t, :], in_=ds[t][:], func=ACT.Square)
+
+        def weave(dst, src, func, bias):
+            nc.scalar.activation(
+                out=dst[:].rearrange("p (c i t) -> p c t i", i=4, t=PACK),
+                in_=src[:].rearrange("p t (c i) -> p c t i", i=4),
+                func=func,
+                bias=bias,
+            )
+
+        def gain_and_quantize(name, src, gain):
+            dst = rounded.tile([P, PACK * M], BF16, name="gained", align_bytes=64, bufs=3)
+            nc.vector.tensor_tensor(
+                dst[:].rearrange("p (m t) -> p m t", t=PACK),
+                src[:].rearrange("p (m t) -> p m t", t=PACK),
+                gain.unsqueeze(1).to_broadcast([P, M, PACK]),
+                ALU.mult,
+            )
+            return quantize(name, dst)
+
+        y = [psum.tile([P, BANK], F32, name="bank") for i in range(8)]
+
+        def x_pass(a, xq):
+            for i in range(8):
+                c0 = H * a + P * i
+                nc.tensor.matmul_mx(
+                    out=y[i][:],
+                    lhsT=w2_w[:, c0 : c0 + P].bitcast(FP4X4),
+                    lhsT_scale=w2_s[a][:, P * i : P * (i + 1)],
+                    rhs=xq[0][:].bitcast(FP8X4),
+                    rhs_scale=xq[1][:],
+                    start=(a == 0),
+                    stop=False,
+                )
+
+        def z_pass(a, zq):
+            for i in range(8):
+                b, t = divmod(i, PACK)
+                codes, scales = w3_q[a, b]
+                nc.tensor.matmul_mx(
+                    out=y[i][:],
+                    lhsT=codes[:, P * t : P * (t + 1)].bitcast(FP8X4),
+                    lhsT_scale=scales[:, P * t : P * (t + 1)],
+                    rhs=zq[0][:].bitcast(FP8X4),
+                    rhs_scale=zq[1][:],
+                    start=False,
+                    stop=(a == 1),
+                )
+
+        gather_left(0)
+        d0 = gather_diff(0)
+        nc.vector.tensor_copy(
+            w2_s[0][:].rearrange("p (g t q) -> p g q t", t=PACK, q=P),
+            w2_sraw[:].rearrange("p (g q t) -> p g q t", t=PACK, q=P),
+        )
+        nc.gpsimd.dma_start(out=w2_s[1][0 : P - 4, :].bitcast(I32), in_=w2_s[0][4:P, :].bitcast(I32))
+        weave(woven[0], left[0], ACT.Gelu_apprx_tanh, 0.0)
+        x_pass(0, gain_and_quantize("x0", woven[0], gx_sb[:, 0, :]))
+        gather_left(1)
+        d1 = gather_diff(1)
+        square(0, d0)
+        w3_q = {}
+        w3_q[0, 0] = quantize("w3_00", round_weight("scalar", w3_raw[0, 0]))
+        w3_q[0, 1] = quantize("w3_01", round_weight("scalar", w3_raw[0, 1]))
+        w3_q[1, 0] = quantize("w3_10", round_weight("scalar", w3_raw[1, 0]))
+        w3_q[1, 1] = quantize("w3_11", round_weight("vector", w3_raw[1, 1]))
+        weave(woven[1], left[1], ACT.Gelu_apprx_tanh, 0.0)
+        x_pass(1, gain_and_quantize("x1", woven[1], gx_sb[:, 1, :]))
+        weave(woven[0], diff[0], ACT.Sqrt, 1.0)
+        z_pass(0, gain_and_quantize("z0", woven[0], gz_sb[:, 0, :]))
+        square(1, d1)
+        weave(woven[1], diff[1], ACT.Sqrt, 1.0)
+        z_pass(1, gain_and_quantize("z1", woven[1], gz_sb[:, 1, :]))
+
+        rows = out.rearrange("(b p t) m -> b t p m", p=P, t=PACK)
+        for i in range(8):
+            b, t = divmod(i, PACK)
+            nc.vector.tensor_tensor(left[b][:, t, :], y[i][:], left[b][:, t, :], ALU.add)
+            nc.sync.dma_start(out=rows[b, t], in_=left[b][:, t, :])

@@ -28,7 +28,7 @@ def tile_list_binaural_fitting_gains_kernel(
     nc = tc.nc
     with ExitStack() as ctx:
         keep = ctx.enter_context(tc.tile_pool(name="keep", bufs=1))
-        raw = ctx.enter_context(tc.tile_pool(name="raw", bufs=5))
+        raw = ctx.enter_context(tc.tile_pool(name="raw", bufs=7))
         rounded = ctx.enter_context(tc.tile_pool(name="rounded", bufs=5))
         psum = ctx.enter_context(tc.psum_pool(name="psum", bufs=8))
 
@@ -65,14 +65,21 @@ def tile_list_binaural_fitting_gains_kernel(
             )
             return t
 
-        def round_weight(engine, src):
-            dst = rounded.tile([P, PACK * PASS], BF16, name="rounded", align_bytes=64)
-            o = dst[:].rearrange("p (t m j) -> p m j t", t=PACK, j=PACK)
+        def round_into(engine, view, src):
             i = src[:].rearrange("p j (m t) -> p m j t", t=PACK)
-            if engine == "scalar":
-                nc.scalar.copy(out=o, in_=i)
+            for u in range(2):
+                pair = slice(2 * u, 2 * u + 2)
+                if engine == "scalar":
+                    nc.scalar.copy(out=view[:, :, :, pair], in_=i[:, :, :, pair])
+                else:
+                    nc.vector.tensor_copy(out=view[:, :, :, pair], in_=i[:, :, :, pair])
+
+        def round_weight(engine, src, own=False):
+            if own:
+                dst = keep.tile([P, PACK * PASS], BF16, name="r11", tag="r11", align_bytes=64)
             else:
-                nc.vector.tensor_copy(out=o, in_=i)
+                dst = rounded.tile([P, PACK * PASS], BF16, name="rounded", align_bytes=64)
+            round_into(engine, dst[:].rearrange("p (t m j) -> p m j t", t=PACK, j=PACK), src)
             return dst
 
         def quantize(name, src):
@@ -130,13 +137,13 @@ def tile_list_binaural_fitting_gains_kernel(
         w1_q[0, 0] = quantize("w1_00", round_weight("scalar", w1_raw[0, 0]))
         nc.vector.tensor_copy(v_w[1][:], tab_w[1][:].indirect(offs_sb[:]))
         nc.vector.tensor_copy(
-            w2_w[:].rearrange("p (g t q) -> p g q t", t=PACK, q=P),
-            w2_raw[:].rearrange("p (g q t) -> p g q t", t=PACK, q=P),
+            w2_w[:].rearrange("p (g t q) -> p g t q", t=PACK, q=P),
+            w2_raw[:].rearrange("p (g q t) -> p g t q", t=PACK, q=P),
         )
         last = rounded.tile([P, PACK * PASS], BF16, name="rounded", align_bytes=64)
         last_view = last[:].rearrange("p (t m j) -> p m j t", t=PACK, j=PACK)
-        nc.scalar.copy(out=last_view[:, 0:64], in_=halves[0][:].rearrange("p j (m t) -> p m j t", t=PACK))
-        nc.vector.tensor_copy(out=last_view[:, 64:128], in_=halves[1][:].rearrange("p j (m t) -> p m j t", t=PACK))
+        round_into("scalar", last_view[:, 0:64], halves[0])
+        round_into("vector", last_view[:, 64:128], halves[1])
         w1_q[1, 0] = quantize("w1_10", last)
 
         h = [keep.tile([P, S], F32, name="h%d" % i, tag="h%d" % i) for i in range(8)]
@@ -160,18 +167,21 @@ def tile_list_binaural_fitting_gains_kernel(
                             start=(a == 0),
                             stop=(a == 1),
                         )
-            for t in range(PACK):
+            return banks
+
+        def evacuate(b, banks, tiles):
+            for t in tiles:
                 for half in range(2):
                     nc.scalar.copy(out=h[PACK * b + t][:, BANK * half : BANK * (half + 1)], in_=banks[t, half][:])
 
         w1_q[0, 1] = quantize("w1_01", round_weight("vector", w1_raw[0, 1]))
-        stage1(0)
-        w1_q[1, 1] = quantize("w1_11", round_weight("scalar", w1_raw[1, 1]))
-        stage1(1)
+        banks = stage1(0)
+        evacuate(0, banks, range(PACK))
+        w1_q[1, 1] = quantize("w1_11", round_weight("scalar", w1_raw[1, 1], True))
+        evacuate(1, stage1(1), range(PACK))
 
         left = [held("left%d" % b, [P, PACK, M], F32) for b in range(2)]
-        diff = [held("diff%d" % b, [P, PACK, M], F32) for b in range(2)]
-        woven = [held("woven%d" % b, [P, M * PACK], F32) for b in range(2)]
+        squares = held("squares", [P, PACK, M], F32)
 
         def gather_left(b):
             for t in range(PACK):
@@ -179,24 +189,29 @@ def tile_list_binaural_fitting_gains_kernel(
 
         def gather_diff(b):
             ds = {}
-            home = "spare" if b == 0 else "h2"
-            for t in (3, 0, 1, 2):
-                ds[t] = keep.tile([P, M], F32, name="d%d%d" % (b, t), tag=home)
+            home = "spare" if b == 0 else "h3"
+            for t in ((0, 1, 2, 3) if b == 0 else (3, 0, 1, 2)):
+                if (b, t) == (0, 1):
+                    ds[t] = keep.tile([P, M], F32, name="d01", tag="r11", align_bytes=64)
+                else:
+                    ds[t] = keep.tile([P, M], F32, name="d%d%d" % (b, t), tag=home)
                 nc.vector.tensor_tensor(ds[t][:], h[PACK * b + t][:].indirect(pos2_sb[:]), left[b][:, t, :], ALU.subtract)
                 home = "h%d" % (PACK * b + t)
             return ds
 
         def square(b, ds):
-            for t in (3, 0, 1, 2):
-                nc.scalar.activation(out=diff[b][:, t, :], in_=ds[t][:], func=ACT.Square)
+            for t in ((0, 1, 2, 3) if b == 0 else (3, 0, 1, 2)):
+                nc.scalar.activation(out=squares[:, t, :], in_=ds[t][:], func=ACT.Square)
 
-        def weave(dst, src, func, bias):
+        def weave(src, func, bias):
+            dst = raw.tile([P, M * PACK], F32, name="raw")
             nc.scalar.activation(
-                out=dst[:].rearrange("p (c i t) -> p c t i", i=4, t=PACK),
-                in_=src[:].rearrange("p t (c i) -> p c t i", i=4),
+                out=dst[:].rearrange("p (c i t) -> p c t i", i=2, t=PACK),
+                in_=src[:].rearrange("p t (c i) -> p c t i", i=2),
                 func=func,
                 bias=bias,
             )
+            return dst
 
         def gain_and_quantize(name, src, gain):
             dst = rounded.tile([P, PACK * M], BF16, name="gained", align_bytes=64, bufs=3)
@@ -240,27 +255,27 @@ def tile_list_binaural_fitting_gains_kernel(
         gather_left(0)
         d0 = gather_diff(0)
         nc.vector.tensor_copy(
-            w2_s[0][:].rearrange("p (g t q) -> p g q t", t=PACK, q=P),
-            w2_sraw[:].rearrange("p (g q t) -> p g q t", t=PACK, q=P),
+            w2_s[0][:].rearrange("p (g t q) -> p g t q", t=PACK, q=P),
+            w2_sraw[:].rearrange("p (g q t) -> p g t q", t=PACK, q=P),
         )
         nc.gpsimd.dma_start(out=w2_s[1][0 : P - 4, :].bitcast(I32), in_=w2_s[0][4:P, :].bitcast(I32))
-        weave(woven[0], left[0], ACT.Gelu_apprx_tanh, 0.0)
-        x_pass(0, gain_and_quantize("x0", woven[0], gx_sb[:, 0, :]))
+        w3_q = {}
+        w3_q[0, 0] = quantize("w3_00", round_weight("scalar", w3_raw[0, 0]))
+        g0 = weave(left[0], ACT.Gelu_apprx_tanh, 0.0)
+        x_pass(0, gain_and_quantize("x0", g0, gx_sb[:, 0, :]))
         gather_left(1)
         d1 = gather_diff(1)
         square(0, d0)
-        w3_q = {}
-        w3_q[0, 0] = quantize("w3_00", round_weight("scalar", w3_raw[0, 0]))
         w3_q[0, 1] = quantize("w3_01", round_weight("scalar", w3_raw[0, 1]))
+        g1 = weave(left[1], ACT.Gelu_apprx_tanh, 0.0)
+        x_pass(1, gain_and_quantize("x1", g1, gx_sb[:, 1, :]))
         w3_q[1, 0] = quantize("w3_10", round_weight("scalar", w3_raw[1, 0]))
         w3_q[1, 1] = quantize("w3_11", round_weight("vector", w3_raw[1, 1]))
-        weave(woven[1], left[1], ACT.Gelu_apprx_tanh, 0.0)
-        x_pass(1, gain_and_quantize("x1", woven[1], gx_sb[:, 1, :]))
-        weave(woven[0], diff[0], ACT.Sqrt, 1.0)
-        z_pass(0, gain_and_quantize("z0", woven[0], gz_sb[:, 0, :]))
+        r0 = weave(squares, ACT.Sqrt, 1.0)
+        z_pass(0, gain_and_quantize("z0", r0, gz_sb[:, 0, :]))
         square(1, d1)
-        weave(woven[1], diff[1], ACT.Sqrt, 1.0)
-        z_pass(1, gain_and_quantize("z1", woven[1], gz_sb[:, 1, :]))
+        r1 = weave(squares, ACT.Sqrt, 1.0)
+        z_pass(1, gain_and_quantize("z1", r1, gz_sb[:, 1, :]))
 
         rows = out.rearrange("(b p t) m -> b t p m", p=P, t=PACK)
         for i in range(8):

@@ -195,7 +195,8 @@ def tile_list_binaural_fitting_gains_kernel(
                     ds[t] = keep.tile([P, M], F32, name="d01", tag="r11", align_bytes=64)
                 else:
                     ds[t] = keep.tile([P, M], F32, name="d%d%d" % (b, t), tag=home)
-                nc.vector.tensor_tensor(ds[t][:], h[PACK * b + t][:].indirect(pos2_sb[:]), left[b][:, t, :], ALU.subtract)
+                nc.vector.tensor_copy(ds[t][:], h[PACK * b + t][:].indirect(pos2_sb[:]))
+                nc.gpsimd.tensor_tensor(ds[t][:], ds[t][:], left[b][:, t, :], ALU.subtract)
                 home = "h%d" % (PACK * b + t)
             return ds
 
@@ -258,7 +259,7 @@ def tile_list_binaural_fitting_gains_kernel(
             w2_s[0][:].rearrange("p (g t q) -> p g t q", t=PACK, q=P),
             w2_sraw[:].rearrange("p (g q t) -> p g t q", t=PACK, q=P),
         )
-        nc.gpsimd.dma_start(out=w2_s[1][0 : P - 4, :].bitcast(I32), in_=w2_s[0][4:P, :].bitcast(I32))
+        nc.sync.dma_start(out=w2_s[1][0 : P - 4, :].bitcast(I32), in_=w2_s[0][4:P, :].bitcast(I32))
         w3_q = {}
         w3_q[0, 0] = quantize("w3_00", round_weight("scalar", w3_raw[0, 0]))
         g0 = weave(left[0], ACT.Gelu_apprx_tanh, 0.0)

@@ -48,7 +48,8 @@ def tile_list_binaural_fitting_gains_kernel(
         w2_s = [held("w2_s%d" % a, [P, H], U8) for a in range(2)]
         gx_sb = held("gx_sb", [P, 2, PACK], F32)
         gz_sb = held("gz_sb", [P, 2, PACK], F32)
-        warm = held("warm", [P, 1], F32)
+
+        zero_bias = held("zero_bias", [P, 1], F32)
 
         def load_scale_rows(queue, tile, scales, row0):
             for q in range(4):
@@ -90,8 +91,8 @@ def tile_list_binaural_fitting_gains_kernel(
 
         for q in range(4):
             nc.vector.memset(tab_s[32 * q : 32 * q + 24, :].bitcast(I32), 0)
-        nc.gpsimd.memset(warm[:], 0.0)
-        nc.scalar.activation(out=warm[:], in_=warm[:], func=ACT.Gelu_apprx_tanh)
+        nc.gpsimd.memset(zero_bias[:], 0.0)
+        nc.scalar.activation(out=zero_bias[:], in_=zero_bias[:], func=ACT.Gelu_apprx_tanh)
         for a in range(2):
             nc.gpsimd.memset(v_s[a][96:P, :].bitcast(I32), 0)
         nc.gpsimd.memset(w2_sraw[:].bitcast(I32), 0)
@@ -102,11 +103,12 @@ def tile_list_binaural_fitting_gains_kernel(
         nc.sync.dma_start(offs_sb[:], offs)
         load_scale_rows(nc.sync, tab_s, tab_scales, 24)
         nc.sync.dma_start(out=tab_w[0][:].bitcast(I32), in_=tab_words[0].bitcast(I32))
+        w1_raw[0, 0] = load_weight(w1, "w1", 0, 0)
         nc.sync.dma_start(
             out=w2_raw[:].bitcast(I32).rearrange("p (a c) -> p a c", a=2),
             in_=w2_words.bitcast(I32).rearrange("a p c -> p a c"),
         )
-        w1_raw[0, 0] = load_weight(w1, "w1", 0, 0)
+        load_scale_rows(nc.sync, w2_sraw, w2_scales, 0)
         nc.sync.dma_start(out=tab_w[1][:].bitcast(I32), in_=tab_words[1].bitcast(I32))
         halves = []
         for u in range(2):
@@ -120,7 +122,6 @@ def tile_list_binaural_fitting_gains_kernel(
         nc.sync.dma_start(pos2_sb[:], pos2)
         w1_raw[0, 1] = load_weight(w1, "w1", 0, 1)
         w1_raw[1, 1] = load_weight(w1, "w1", 1, 1)
-        load_scale_rows(nc.sync, w2_sraw, w2_scales, 0)
         nc.sync.dma_start(out=gx_sb[:], in_=gx.rearrange("(b p t) -> p b t", p=P, t=PACK))
         nc.sync.dma_start(out=gz_sb[:], in_=gz.rearrange("(b p t) -> p b t", p=P, t=PACK))
         for a in range(2):
@@ -140,6 +141,11 @@ def tile_list_binaural_fitting_gains_kernel(
             w2_w[:].rearrange("p (g t q) -> p g t q", t=PACK, q=P),
             w2_raw[:].rearrange("p (g q t) -> p g t q", t=PACK, q=P),
         )
+        nc.vector.tensor_copy(
+            w2_s[0][:].rearrange("p (g t q) -> p g t q", t=PACK, q=P),
+            w2_sraw[:].rearrange("p (g q t) -> p g t q", t=PACK, q=P),
+        )
+        nc.gpsimd.dma_start(out=w2_s[1][0 : P - 4, :].bitcast(I32), in_=w2_s[0][4:P, :].bitcast(I32))
         last = rounded.tile([P, PACK * PASS], BF16, name="rounded", align_bytes=64)
         last_view = last[:].rearrange("p (t m j) -> p m j t", t=PACK, j=PACK)
         round_into("scalar", last_view[:, 0:64], halves[0])
@@ -153,9 +159,9 @@ def tile_list_binaural_fitting_gains_kernel(
             for t in range(PACK):
                 for half in range(2):
                     banks[t, half] = psum.tile([P, BANK], F32, name="bank")
-            for a in range(2):
-                codes, scales = w1_q[a, b]
-                for t in range(PACK):
+            for t in range(PACK):
+                for a in range(2):
+                    codes, scales = w1_q[a, b]
                     for half in range(2):
                         cols = slice(BANK * half, BANK * (half + 1))
                         nc.tensor.matmul_mx(
@@ -195,8 +201,7 @@ def tile_list_binaural_fitting_gains_kernel(
                     ds[t] = keep.tile([P, M], F32, name="d01", tag="r11", align_bytes=64)
                 else:
                     ds[t] = keep.tile([P, M], F32, name="d%d%d" % (b, t), tag=home)
-                nc.vector.tensor_copy(ds[t][:], h[PACK * b + t][:].indirect(pos2_sb[:]))
-                nc.gpsimd.tensor_tensor(ds[t][:], ds[t][:], left[b][:, t, :], ALU.subtract)
+                nc.vector.tensor_tensor(ds[t][:], h[PACK * b + t][:].indirect(pos2_sb[:]), left[b][:, t, :], ALU.subtract)
                 home = "h%d" % (PACK * b + t)
             return ds
 
@@ -204,25 +209,36 @@ def tile_list_binaural_fitting_gains_kernel(
             for t in ((0, 1, 2, 3) if b == 0 else (3, 0, 1, 2)):
                 nc.scalar.activation(out=squares[:, t, :], in_=ds[t][:], func=ACT.Square)
 
-        def weave(src, func, bias):
+        def weave(src, func, bias, parts=1):
             dst = raw.tile([P, M * PACK], F32, name="raw")
-            nc.scalar.activation(
-                out=dst[:].rearrange("p (c i t) -> p c t i", i=2, t=PACK),
-                in_=src[:].rearrange("p t (c i) -> p c t i", i=2),
-                func=func,
-                bias=bias,
-            )
+            for u in range(parts):
+                cs = slice(u * 256 // parts, (u + 1) * 256 // parts)
+                nc.scalar.activation(
+                    out=dst[:].rearrange("p (c i t) -> p c t i", i=2, t=PACK)[:, cs],
+                    in_=src[:].rearrange("p t (c i) -> p c t i", i=2)[:, cs],
+                    func=func,
+                    bias=bias,
+                )
             return dst
 
         def gain_and_quantize(name, src, gain):
             dst = rounded.tile([P, PACK * M], BF16, name="gained", align_bytes=64, bufs=3)
-            nc.vector.tensor_tensor(
-                dst[:].rearrange("p (m t) -> p m t", t=PACK),
-                src[:].rearrange("p (m t) -> p m t", t=PACK),
-                gain.unsqueeze(1).to_broadcast([P, M, PACK]),
-                ALU.mult,
-            )
-            return quantize(name, dst)
+            for u in range(2):
+                nc.vector.tensor_tensor(
+                    dst[:].rearrange("p (m t) -> p m t", t=PACK)[:, 256 * u : 256 * (u + 1)],
+                    src[:].rearrange("p (m t) -> p m t", t=PACK)[:, 256 * u : 256 * (u + 1)],
+                    gain.unsqueeze(1).to_broadcast([P, M // 2, PACK]),
+                    ALU.mult,
+                )
+            codes = held(name + "_c", [P, M], U32)
+            scales = held(name + "_s", [P, M], U8)
+            for u in range(2):
+                nc.vector.quantize_mx(
+                    out=codes[:, 256 * u : 256 * (u + 1)].bitcast(FP8X4),
+                    scales=scales[:, 256 * u : 256 * (u + 1)],
+                    in_=dst[:, 1024 * u : 1024 * (u + 1)],
+                )
+            return codes, scales
 
         y = [psum.tile([P, BANK], F32, name="bank") for i in range(8)]
 
@@ -255,27 +271,22 @@ def tile_list_binaural_fitting_gains_kernel(
 
         gather_left(0)
         d0 = gather_diff(0)
-        nc.vector.tensor_copy(
-            w2_s[0][:].rearrange("p (g t q) -> p g t q", t=PACK, q=P),
-            w2_sraw[:].rearrange("p (g q t) -> p g t q", t=PACK, q=P),
-        )
-        nc.sync.dma_start(out=w2_s[1][0 : P - 4, :].bitcast(I32), in_=w2_s[0][4:P, :].bitcast(I32))
         w3_q = {}
         w3_q[0, 0] = quantize("w3_00", round_weight("scalar", w3_raw[0, 0]))
-        g0 = weave(left[0], ACT.Gelu_apprx_tanh, 0.0)
+        g0 = weave(left[0], ACT.Gelu_apprx_tanh, zero_bias[:])
         x_pass(0, gain_and_quantize("x0", g0, gx_sb[:, 0, :]))
         gather_left(1)
         d1 = gather_diff(1)
         square(0, d0)
         w3_q[0, 1] = quantize("w3_01", round_weight("scalar", w3_raw[0, 1]))
-        g1 = weave(left[1], ACT.Gelu_apprx_tanh, 0.0)
+        g1 = weave(left[1], ACT.Gelu_apprx_tanh, zero_bias[:])
         x_pass(1, gain_and_quantize("x1", g1, gx_sb[:, 1, :]))
         w3_q[1, 0] = quantize("w3_10", round_weight("scalar", w3_raw[1, 0]))
         w3_q[1, 1] = quantize("w3_11", round_weight("vector", w3_raw[1, 1]))
         r0 = weave(squares, ACT.Sqrt, 1.0)
         z_pass(0, gain_and_quantize("z0", r0, gz_sb[:, 0, :]))
         square(1, d1)
-        r1 = weave(squares, ACT.Sqrt, 1.0)
+        r1 = weave(squares, ACT.Sqrt, 1.0, 2)
         z_pass(1, gain_and_quantize("z1", r1, gz_sb[:, 1, :]))
 
         rows = out.rearrange("(b p t) m -> b t p m", p=P, t=PACK)

from contextlib import ExitStack

import concourse.mybir as mybir

K, H, T, S, M = 1024, 1024, 4096, 1024, 512
FLOPS = 2 * K * H * S + 2 * 2 * H * H * M

F32 = mybir.dt.float32
BF16 = mybir.dt.bfloat16
I32 = mybir.dt.int32
U32 = mybir.dt.uint32
U16 = mybir.dt.uint16
U8 = mybir.dt.uint8
FP8X4 = mybir.dt.float8_e4m3fn_x4
FP4X4 = mybir.dt.float4_e2m1fn_x4
ACT = mybir.ActivationFunctionType
ALU = mybir.AluOpType

P = 128
PACK = 4
PASS = P * PACK
BANK = 512


def tile_list_binaural_fitting_gains_kernel(
    tc, tab_words, tab_scales, offs, pos1, pos2, w1, w2_words, w2_scales, w3, gx, gz, out
):
    nc = tc.nc
    with ExitStack() as ctx:
        keep = ctx.enter_context(tc.tile_pool(name="keep", bufs=1))
        raw = ctx.enter_context(tc.tile_pool(name="raw", bufs=7))
        rounded = ctx.enter_context(tc.tile_pool(name="rounded", bufs=5))
        psum = ctx.enter_context(tc.psum_pool(name="psum", bufs=8))

        def held(name, shape, dtype):
            return keep.tile(shape, dtype, name=name, align_bytes=64)

        offs_sb = keep.tile([P, S // 16], U16, name="offs_sb")
        pos1_sb = keep.tile([P, M // 16], U16, name="pos1_sb")
        pos2_sb = keep.tile([P, M // 16], U16, name="pos2_sb")
        tab_w = [held("tab_w%d" % a, [P, T], U16) for a in range(2)]
        tab_s = held("tab_s", [P, T], U8)
        v_w = [held("v_w%d" % a, [P, S], U16) for a in range(2)]
        v_s = [held("v_s%d" % a, [P, S], U8) for a in range(2)]
        w2_raw = held("w2_raw", [P, 2 * H], U16)
        w2_w = held("w2_w", [P, 2 * H], U16)
        w2_sraw = held("w2_sraw", [P, H], U8)
        w2_s = [held("w2_s%d" % a, [P, H], U8) for a in range(2)]
        gx_sb = held("gx_sb", [P, 2, PACK], F32)
        gz_sb = held("gz_sb", [P, 2, PACK], F32)

        zero_bias = held("zero_bias", [P, 1], F32)

        def load_scale_rows(queue, tile, scales, row0):
            for q in range(4):
                queue.dma_start(
                    out=tile[32 * q + row0 : 32 * q + row0 + 8, :].bitcast(I32),
                    in_=scales[:, 4 * q : 4 * q + 4, :].bitcast(I32),
                )

        def load_weight(w, name, a, b):
            t = raw.tile([P, PACK, PASS], F32, name="raw")
            nc.sync.dma_start(
                out=t[:],
                in_=w[PASS * a : PASS * (a + 1), PASS * b : PASS * (b + 1)].rearrange("(p j) c -> p j c", j=PACK),
            )
            return t

        def round_into(engine, view, src):
            i = src[:].rearrange("p j (m t) -> p m j t", t=PACK)
            for u in range(2):
                pair = slice(2 * u, 2 * u + 2)
                if engine == "scalar":
                    nc.scalar.copy(out=view[:, :, :, pair], in_=i[:, :, :, pair])
                else:
                    nc.vector.tensor_copy(out=view[:, :, :, pair], in_=i[:, :, :, pair])

        def round_weight(engine, src, own=False):
            if own:
                dst = keep.tile([P, PACK * PASS], BF16, name="r11", tag="r11", align_bytes=64)
            else:
                dst = rounded.tile([P, PACK * PASS], BF16, name="rounded", align_bytes=64)
            round_into(engine, dst[:].rearrange("p (t m j) -> p m j t", t=PACK, j=PACK), src)
            return dst

        def quantize(name, src):
            codes = held(name + "_c", [P, PASS], U32)
            scales = held(name + "_s", [P, PASS], U8)
            nc.vector.quantize_mx(out=codes[:].bitcast(FP8X4), scales=scales[:], in_=src[:])
            return codes, scales

        for q in range(4):
            nc.vector.memset(tab_s[32 * q : 32 * q + 24, :].bitcast(I32), 0)
        nc.gpsimd.memset(zero_bias[:], 0.0)
        nc.scalar.activation(out=zero_bias[:], in_=zero_bias[:], func=ACT.Gelu_apprx_tanh)
        for a in range(2):
            nc.gpsimd.memset(v_s[a][96:P, :].bitcast(I32), 0)
        nc.gpsimd.memset(w2_sraw[:].bitcast(I32), 0)
        nc.gpsimd.memset(w2_s[1][96:P, :].bitcast(I32), 0)

        w1_raw = {}
        w3_raw = {}
        nc.sync.dma_start(offs_sb[:], offs)
        load_scale_rows(nc.sync, tab_s, tab_scales, 24)
        nc.sync.dma_start(out=tab_w[0][:].bitcast(I32), in_=tab_words[0].bitcast(I32))
        w1_raw[0, 0] = load_weight(w1, "w1", 0, 0)
        nc.sync.dma_start(
            out=w2_raw[:].bitcast(I32).rearrange("p (a c) -> p a c", a=2),
            in_=w2_words.bitcast(I32).rearrange("a p c -> p a c"),
        )
        load_scale_rows(nc.sync, w2_sraw, w2_scales, 0)
        nc.sync.dma_start(out=tab_w[1][:].bitcast(I32), in_=tab_words[1].bitcast(I32))
        halves = []
        for u in range(2):
            piece = held("w1_half%d" % u, [P, PACK, PASS // 2], F32)
            nc.sync.dma_start(
                out=piece[:],
                in_=w1[PASS : 2 * PASS, 256 * u : 256 * (u + 1)].rearrange("(p j) c -> p j c", j=PACK),
            )
            halves.append(piece)
        nc.sync.dma_start(pos1_sb[:], pos1)
        nc.sync.dma_start(pos2_sb[:], pos2)
        w1_raw[0, 1] = load_weight(w1, "w1", 0, 1)
        w1_raw[1, 1] = load_weight(w1, "w1", 1, 1)
        nc.sync.dma_start(out=gx_sb[:], in_=gx.rearrange("(b p t) -> p b t", p=P, t=PACK))
        nc.sync.dma_start(out=gz_sb[:], in_=gz.rearrange("(b p t) -> p b t", p=P, t=PACK))
        for a in range(2):
            for b in range(2):
                w3_raw[a, b] = load_weight(w3, "w3", a, b)

        picked_s = held("picked_s", [P, S], U8)
        nc.vector.tensor_copy(picked_s[:], tab_s[:].indirect(offs_sb[:]))
        for a in range(2):
            row0 = 24 + 4 * a
            nc.scalar.dma_start(out=v_s[a][0 : P - row0, :].bitcast(I32), in_=picked_s[row0:P, :].bitcast(I32))
        w1_q = {}
        nc.vector.tensor_copy(v_w[0][:], tab_w[0][:].indirect(offs_sb[:]))
        w1_q[0, 0] = quantize("w1_00", round_weight("scalar", w1_raw[0, 0]))
        nc.vector.tensor_copy(v_w[1][:], tab_w[1][:].indirect(offs_sb[:]))
        nc.vector.tensor_copy(
            w2_w[:].rearrange("p (g t q) -> p g t q", t=PACK, q=P),
            w2_raw[:].rearrange("p (g q t) -> p g t q", t=PACK, q=P),
        )
        nc.vector.tensor_copy(
            w2_s[0][:].rearrange("p (g t q) -> p g t q", t=PACK, q=P),
            w2_sraw[:].rearrange("p (g q t) -> p g t q", t=PACK, q=P),
        )
        nc.gpsimd.dma_start(out=w2_s[1][0 : P - 4, :].bitcast(I32), in_=w2_s[0][4:P, :].bitcast(I32))
        last = rounded.tile([P, PACK * PASS], BF16, name="rounded", align_bytes=64)
        last_view = last[:].rearrange("p (t m j) -> p m j t", t=PACK, j=PACK)
        round_into("scalar", last_view[:, 0:64], halves[0])
        round_into("vector", last_view[:, 64:128], halves[1])
        w1_q[1, 0] = quantize("w1_10", last)

        h = [keep.tile([P, S], F32, name="h%d" % i, tag="h%d" % i) for i in range(8)]

        def stage1(b):
            banks = {}
            for t in range(PACK):
                for half in range(2):
                    banks[t, half] = psum.tile([P, BANK], F32, name="bank")
            for t in range(PACK):
                for a in range(2):
                    codes, scales = w1_q[a, b]
                    for half in range(2):
                        cols = slice(BANK * half, BANK * (half + 1))
                        nc.tensor.matmul_mx(
                            out=banks[t, half][:],
                            lhsT=codes[:, P * t : P * (t + 1)].bitcast(FP8X4),
                            lhsT_scale=scales[:, P * t : P * (t + 1)],
                            rhs=v_w[a][:, cols].bitcast(FP4X4),
                            rhs_scale=v_s[a][:, cols],
                            start=(a == 0),
                            stop=(a == 1),
                        )
            return banks

        def evacuate(b, banks, tiles):
            for t in tiles:
                for half in range(2):
                    nc.scalar.copy(out=h[PACK * b + t][:, BANK * half : BANK * (half + 1)], in_=banks[t, half][:])

        w1_q[0, 1] = quantize("w1_01", round_weight("vector", w1_raw[0, 1]))
        banks = stage1(0)
        evacuate(0, banks, range(PACK))
        w1_q[1, 1] = quantize("w1_11", round_weight("scalar", w1_raw[1, 1], True))
        evacuate(1, stage1(1), range(PACK))

        left = [held("left%d" % b, [P, PACK, M], F32) for b in range(2)]
        squares = held("squares", [P, PACK, M], F32)

        def gather_left(b):
            for t in range(PACK):
                nc.vector.tensor_copy(left[b][:, t, :], h[PACK * b + t][:].indirect(pos1_sb[:]))

        def gather_diff(b):
            ds = {}
            home = "spare" if b == 0 else "h3"
            for t in ((0, 1, 2, 3) if b == 0 else (3, 0, 1, 2)):
                if (b, t) == (0, 1):
                    ds[t] = keep.tile([P, M], F32, name="d01", tag="r11", align_bytes=64)
                else:
                    ds[t] = keep.tile([P, M], F32, name="d%d%d" % (b, t), tag=home)
                nc.vector.tensor_tensor(ds[t][:], h[PACK * b + t][:].indirect(pos2_sb[:]), left[b][:, t, :], ALU.subtract)
                home = "h%d" % (PACK * b + t)
            return ds

        def square(b, ds):
            for t in ((0, 1, 2, 3) if b == 0 else (3, 0, 1, 2)):
                nc.scalar.activation(out=squares[:, t, :], in_=ds[t][:], func=ACT.Square)

        def weave(src, func, bias, parts=1):
            dst = raw.tile([P, M * PACK], F32, name="raw")
            for u in range(parts):
                cs = slice(u * 256 // parts, (u + 1) * 256 // parts)
                nc.scalar.activation(
                    out=dst[:].rearrange("p (c i t) -> p c t i", i=2, t=PACK)[:, cs],
                    in_=src[:].rearrange("p t (c i) -> p c t i", i=2)[:, cs],
                    func=func,
                    bias=bias,
                )
            return dst

        def gain_and_quantize(name, src, gain):
            dst = rounded.tile([P, PACK * M], BF16, name="gained", align_bytes=64, bufs=3)
            for u in range(2):
                nc.vector.tensor_tensor(
                    dst[:].rearrange("p (m t) -> p m t", t=PACK)[:, 256 * u : 256 * (u + 1)],
                    src[:].rearrange("p (m t) -> p m t", t=PACK)[:, 256 * u : 256 * (u + 1)],
                    gain.unsqueeze(1).to_broadcast([P, M // 2, PACK]),
                    ALU.mult,
                )
            codes = held(name + "_c", [P, M], U32)
            scales = held(name + "_s", [P, M], U8)
            for u in range(2):
                nc.vector.quantize_mx(
                    out=codes[:, 256 * u : 256 * (u + 1)].bitcast(FP8X4),
                    scales=scales[:, 256 * u : 256 * (u + 1)],
                    in_=dst[:, 1024 * u : 1024 * (u + 1)],
                )
            return codes, scales

        y = [psum.tile([P, BANK], F32, name="bank") for i in range(8)]

        def x_pass(a, xq):
            for i in range(8):
                c0 = H * a + P * i
                nc.tensor.matmul_mx(
                    out=y[i][:],
                    lhsT=w2_w[:, c0 : c0 + P].bitcast(FP4X4),
                    lhsT_scale=w2_s[a][:, P * i : P * (i + 1)],
                    rhs=xq[0][:].bitcast(FP8X4),
                    rhs_scale=xq[1][:],
                    start=(a == 0),
                    stop=False,
                )

        def z_pass(a, zq):
            for i in range(8):
                b, t = divmod(i, PACK)
                codes, scales = w3_q[a, b]
                nc.tensor.matmul_mx(
                    out=y[i][:],
                    lhsT=codes[:, P * t : P * (t + 1)].bitcast(FP8X4),
                    lhsT_scale=scales[:, P * t : P * (t + 1)],
                    rhs=zq[0][:].bitcast(FP8X4),
                    rhs_scale=zq[1][:],
                    start=False,
                    stop=(a == 1),
                )

        gather_left(0)
        d0 = gather_diff(0)
        w3_q = {}
        w3_q[0, 0] = quantize("w3_00", round_weight("scalar", w3_raw[0, 0]))
        g0 = weave(left[0], ACT.Gelu_apprx_tanh, zero_bias[:])
        x_pass(0, gain_and_quantize("x0", g0, gx_sb[:, 0, :]))
        gather_left(1)
        d1 = gather_diff(1)
        square(0, d0)
        w3_q[0, 1] = quantize("w3_01", round_weight("scalar", w3_raw[0, 1]))
        g1 = weave(left[1], ACT.Gelu_apprx_tanh, zero_bias[:])
        x_pass(1, gain_and_quantize("x1", g1, gx_sb[:, 1, :]))
        w3_q[1, 0] = quantize("w3_10", round_weight("scalar", w3_raw[1, 0]))
        w3_q[1, 1] = quantize("w3_11", round_weight("vector", w3_raw[1, 1]))
        r0 = weave(squares, ACT.Sqrt, 1.0)
        z_pass(0, gain_and_quantize("z0", r0, gz_sb[:, 0, :]))
        square(1, d1)
        r1 = weave(squares, ACT.Sqrt, 1.0, 2)
        z_pass(1, gain_and_quantize("z1", r1, gz_sb[:, 1, :]))

        rows = out.rearrange("(b p t) m -> b t p m", p=P, t=PACK)
        for i in range(8):
            b, t = divmod(i, PACK)
            nc.vector.tensor_tensor(left[b][:, t, :], y[i][:], left[b][:, t, :], ALU.add)
            nc.sync.dma_start(out=rows[b, t], in_=left[b][:, t, :])
